import numpy as np
import ml_dtypes


def mxq(x, axis, fmt="e4m3"):
    dtype, down = {"e4m3": (ml_dtypes.float8_e4m3fn, 7), "e5m2": (ml_dtypes.float8_e5m2, 14)}[fmt]
    v = np.moveaxis(np.asarray(x, np.float32).astype(ml_dtypes.bfloat16).astype(np.float64), axis, -1)
    blocks = v.reshape(v.shape[:-1] + (-1, 32))
    amax = np.abs(blocks).max(-1, keepdims=True)
    byte = np.maximum(np.where(amax > 0, np.frexp(amax)[1] - 1 + 127, 0) - down, 1)
    scale = np.exp2(byte - 127.0)
    codes = (blocks / scale).astype(np.float32).astype(dtype).astype(np.float64)
    return np.moveaxis((codes * scale).reshape(v.shape), -1, axis)


WIDE = False


def mx_kscale(k):
    if not WIDE:
        return np.ones(k)
    levels = np.array([10, -10, 5, -5, 0])
    if k % 512:
        return np.exp2(np.random.permutation(np.resize(levels, k // 32))).repeat(32)
    a = np.empty((k // 512, 16))
    for p in range(k // 512):
        a[p, :8] = np.random.permutation(np.resize(levels, 8))
        for g in range(8):
            far = levels[np.abs(levels - a[p, g]) >= 10]
            a[p, g + 8] = far[np.random.randint(len(far))]
    return np.exp2(a.ravel()).repeat(32)


def f64(x):
    return np.asarray(x).astype(np.float64)


def striped(idx):
    return np.tile(idx.reshape(-1, 16).T, (8, 1)).astype(np.uint16)


def unstriped(offs):
    return offs[:16].T.reshape(-1).astype(np.int64)


def striped8(idx):
    return np.concatenate([x.reshape(-1, 16).T for x in idx]).astype(np.uint16)


def runs(offs, k):
    lists = np.stack([offs[16 * r : 16 * r + 16].T.reshape(-1) for r in range(8)]).astype(np.int64)
    return lists[np.arange(k) % 512 // 64]


def pack_weight(w):
    k, n = w.shape
    w = f64(np.asarray(w, np.float32).astype(ml_dtypes.bfloat16)).reshape(k // 32, 32, n)
    amax = np.abs(w).max(1)
    byte = np.clip(np.where(amax > 0, np.frexp(amax)[1] - 1 + 127 - 7, 1), 1, 254)
    scaled = (w * np.exp2(127.0 - byte)[:, None, :]).reshape(k, n).astype(np.float32)
    words = np.ascontiguousarray(scaled.reshape(k // 512, 128, 4, n).transpose(0, 1, 3, 2)).astype(ml_dtypes.float8_e4m3fn).view(np.uint8)
    return words, np.ascontiguousarray(byte.astype(np.uint8).reshape(k // 512, 16, n))


def unpack_weight(words, scales):
    g, p, n, _ = words.shape
    vals = np.ascontiguousarray(words).view(ml_dtypes.float8_e4m3fn).astype(np.float64) * np.repeat(np.exp2(scales.astype(np.float64) - 127.0), 8, axis=1)[..., None]
    return vals.transpose(0, 1, 3, 2).reshape(g * 512, n)


K, T, S, H, C = 512, 2048, 256, 512, 512


def setup_inputs():
    n = np.random.standard_normal
    s = mx_kscale(K)[:, None]
    packed_xT = pack_weight(n((K, T)) * s)
    return {
        "x_words": packed_xT[0],
        "x_scales": packed_xT[1],
        "w1": (n((K, H)) / np.sqrt(K) / s).astype(np.float32),
        "tau": np.random.uniform(0.3, 0.9, (H, 1)).astype(np.float32),
        "gs": (np.random.uniform(0.5, 1.5, (K, 1)) / s).astype(np.float32),
        "tau2": np.random.uniform(0.3, 0.9, (C, 1)).astype(np.float32),
        "offs": striped(np.random.permutation(T)[:S]),
        "n1": striped8(np.stack([np.random.permutation(S) for _ in range(8)])),
        "n2": striped8(np.stack([np.random.permutation(S) for _ in range(8)])),
        "ca": striped(np.random.permutation(T)[:C]),
        "cb": striped(np.random.permutation(T)[:C]),
        "n3": striped8(np.stack([np.random.permutation(S) for _ in range(8)])),
        "n4": striped8(np.stack([np.random.permutation(S) for _ in range(8)])),
    }


def reference(x_words, x_scales, w1, tau, gs, tau2, offs, n1, n2, ca, cb, n3, n4):
    x_ca = unpack_weight(x_words, x_scales)[:, unstriped(ca)]
    xq = unpack_weight(x_words, x_scales)[:, unstriped(offs)]
    y = mxq(f64(w1), 0, "e4m3").T @ xq
    low = y.min(axis=1, keepdims=True)
    ea = np.exp(f64(tau) * (low - (y[np.arange(H)[:, None], runs(n1, H)])))
    z = f64(gs) * (y - (2.0 * (ea * (y[np.arange(H)[:, None], runs(n2, H)]))))
    zq = mxq(z, 0, "e4m3")
    a = 0.0625 * (x_ca.T @ zq)
    x_cb = unpack_weight(x_words, x_scales)[:, unstriped(cb)]
    b = 0.0625 * (x_cb.T @ zq)
    top = b.max(axis=1, keepdims=True)
    ea2 = np.exp(f64(tau2) * (b[np.arange(C)[:, None], runs(n3, C)] - top))
    return (0.5 * (a - (a[np.arange(C)[:, None], runs(n4, C)]))) / (ea2 + 0.25)

@@ -1,0 +1,241 @@
+from contextlib import ExitStack
+
+import concourse.mybir as mybir
+
+K, T, S, H, C = 512, 2048, 256, 512, 512
+FLOPS = 2 * K * S * (H + 2 * C)
+
+F32 = mybir.dt.float32
+BF16 = mybir.dt.bfloat16
+I32 = mybir.dt.int32
+U32 = mybir.dt.uint32
+U16 = mybir.dt.uint16
+U8 = mybir.dt.uint8
+FP8X4 = mybir.dt.float8_e4m3fn_x4
+ALU = mybir.AluOpType
+ACT = mybir.ActivationFunctionType
+
+P = 128
+PACK = 4
+HALF = S // 2
+SCALAR_SHARE = 22
+
+
+def tile_picked_ccmpqxbebz_none_p_kernel(
+    tc, x_words, x_scales, w1, tau, gs, tau2, offs, n1, n2, ca, cb, n3, n4, out
+):
+    nc = tc.nc
+    with ExitStack() as ctx:
+        lists = ctx.enter_context(tc.tile_pool(name="lists", bufs=1))
+        keep = ctx.enter_context(tc.tile_pool(name="keep", bufs=1))
+        ring = ctx.enter_context(tc.tile_pool(name="ring", bufs=3))
+        psum = ctx.enter_context(tc.psum_pool(name="psum", bufs=1))
+
+        def load_list(src, name):
+            tl = lists.tile(list(src.shape), U16, name=name)
+            nc.sync.dma_start(tl[:], src)
+            return tl
+
+        def load_rows(src, name):
+            tl = keep.tile([P, PACK], F32, name=name)
+            nc.sync.dma_start(tl[:], src.rearrange("(p t) o -> p (t o)", t=PACK))
+            return tl
+
+        table_bytes = keep.tile([P, T], U8, name="table_bytes", align_bytes=64)
+        nc.vector.memset(table_bytes[:].bitcast(I32), 0)
+
+        offs_sb = load_list(offs, "offs_sb")
+        cb_sb = load_list(cb, "cb_sb")
+        table_words = keep.tile([P, T], U32, name="table_words", align_bytes=64)
+        nc.sync.dma_start(table_words[:].bitcast(I32), x_words[0].rearrange("p n r -> p (n r)").bitcast(I32))
+        for r in range(PACK):
+            nc.sync.dma_start(table_bytes[r:P:32, :].bitcast(I32), x_scales[0, r:16:PACK, :].bitcast(I32))
+
+        w_rows = w1.rearrange("(p j) c -> p j c", j=PACK)
+        w_raw = []
+        for u in range(2):
+            raw = keep.tile([P, PACK, H // 2], F32, name="w_raw%d" % u)
+            nc.sync.dma_start(raw[:], w_rows[:, :, u * (H // 2) : (u + 1) * (H // 2)])
+            w_raw.append(raw)
+
+        n2_sb = load_list(n2, "n2_sb")
+        n1_sb = load_list(n1, "n1_sb")
+        tau_sb = load_rows(tau, "tau_sb")
+        gs_sb = load_rows(gs, "gs_sb")
+        n3_sb = load_list(n3, "n3_sb")
+        tau2_sb = load_rows(tau2, "tau2_sb")
+        ca_sb = load_list(ca, "ca_sb")
+        n4_sb = load_list(n4, "n4_sb")
+
+        def scaled(src, factor, name):
+            tl = keep.tile([P, PACK], F32, name=name)
+            nc.gpsimd.tensor_scalar(tl[:], src[:], factor, 0.0, ALU.mult, ALU.add)
+            return tl
+
+        neg_tau = scaled(tau_sb, -1.0, "neg_tau")
+        neg_2gs = scaled(gs_sb, -2.0, "neg_2gs")
+        neg_tau2 = scaled(tau2_sb, -1.0, "neg_tau2")
+
+        xq_words = keep.tile([P, S], U32, name="xq_words", align_bytes=64)
+        xq_bytes = keep.tile([P, S], U8, name="xq_bytes", tag="picked_bytes", align_bytes=64)
+        nc.vector.tensor_copy(xq_words[:], table_words[:].indirect(offs_sb[:]))
+        nc.vector.tensor_copy(xq_bytes[:], table_bytes[:].indirect(offs_sb[:]))
+
+        def pick_words(list_sb, name):
+            words = keep.tile([P, PACK, P], U32, name=name, tag="pair_words", align_bytes=64)
+            nc.vector.tensor_copy(words[:].rearrange("p t m -> p m t"), table_words[:].indirect(list_sb[:]))
+            return words
+
+        def pick_bytes(list_sb, name):
+            scale_bytes = keep.tile([P, PACK, P], U8, name=name, tag="picked_bytes", align_bytes=64)
+            nc.vector.tensor_copy(scale_bytes[:].rearrange("p t m -> p m t"), table_bytes[:].indirect(list_sb[:]))
+            return scale_bytes
+
+        cb_words = pick_words(cb_sb, "cb_words")
+
+        w_grouped = keep.tile([P, PACK, P, PACK], BF16, name="w_grouped", align_bytes=64)
+
+        def deal_views(u, m0, m1):
+            dst = w_grouped[:, :, u * 64 + m0 : u * 64 + m1, :].rearrange("p t m j -> p m j t")
+            src = w_raw[u][:, :, PACK * m0 : PACK * m1].rearrange("p j (m t) -> p m j t", t=PACK)
+            return dst, src
+
+        nc.scalar.activation(*deal_views(0, 0, 64), ACT.Copy)
+        nc.scalar.activation(*deal_views(1, 0, SCALAR_SHARE), ACT.Copy)
+        nc.vector.tensor_copy(*deal_views(1, SCALAR_SHARE, 64))
+        w_codes = keep.tile([P, PACK, P], U32, name="w_codes", align_bytes=64)
+        w_bytes = keep.tile([P, PACK, P], U8, name="w_bytes", align_bytes=64)
+
+        low = keep.tile([P, PACK], F32, name="low")
+        bias1 = keep.tile([P, PACK], F32, name="bias1")
+        y_sb = []
+        for t in range(PACK):
+            nc.vector.quantize_mx(
+                out=w_codes[:, t, :].bitcast(FP8X4),
+                scales=w_bytes[:, t, :],
+                in_=w_grouped[:, t, :, :].rearrange("p m j -> p (m j)"),
+            )
+            y_ps = psum.tile([P, S], F32, name="y_ps%d" % t, tag="ya%d" % t)
+            nc.tensor.matmul_mx(
+                out=y_ps[:],
+                lhsT=w_codes[:, t, :].bitcast(FP8X4),
+                lhsT_scale=w_bytes[:, t, :],
+                rhs=xq_words[:].bitcast(FP8X4),
+                rhs_scale=xq_bytes[:],
+                start=True,
+                stop=True,
+            )
+            y_t = keep.tile([P, S], F32, name="y_sb%d" % t)
+            nc.vector.tensor_scalar(y_t[:], y_ps[:], 1.0, None, ALU.mult, ALU.min, accum_out=low[:, t : t + 1])
+            nc.vector.tensor_tensor(bias1[:, t : t + 1], low[:, t : t + 1], tau_sb[:, t : t + 1], ALU.mult)
+            y_sb.append(y_t)
+
+        cb_bytes = pick_bytes(cb_sb, "cb_bytes")
+
+        b_win = [keep.tile([P, 2 * S], F32, name="b_win%d" % t) for t in range(PACK)]
+        z_codes = keep.tile([P, S], U32, name="z_codes", align_bytes=64)
+        z_bytes = keep.tile([P, S], U8, name="z_bytes", align_bytes=64)
+        b_ps = [psum.tile([P, S], F32, name="b_ps%d" % t) for t in range(PACK)]
+        top_part = keep.tile([P, 1], F32, name="top_part")
+        top = keep.tile([P, PACK], F32, name="top")
+        bias2 = keep.tile([P, PACK], F32, name="bias2")
+
+        def score(ps, words, scale_bytes, t, cols):
+            nc.tensor.matmul_mx(
+                out=ps[:, cols],
+                lhsT=words[:, t, :].bitcast(FP8X4),
+                lhsT_scale=scale_bytes[:, t, :],
+                rhs=z_codes[:, cols].bitcast(FP8X4),
+                rhs_scale=z_bytes[:, cols],
+                start=True,
+                stop=True,
+            )
+
+        for h in range(2):
+            cols = slice(h * HALF, (h + 1) * HALF)
+            lcols = slice(h * HALF // 16, (h + 1) * HALF // 16)
+            z_f32 = keep.tile([P, PACK, HALF], F32, name="z_f32_%d" % h)
+            z_bf = keep.tile([P, HALF, PACK], BF16, name="z_bf_%d" % h, align_bytes=64)
+            for t in range(PACK):
+                pull = b_win[t][:, S + h * HALF : S + (h + 1) * HALF]
+                y_n2 = ring.tile([P, HALF], F32, name="y_n2")
+                ea = ring.tile([P, HALF], F32, name="ea")
+                nc.scalar.activation(y_n2[:], y_sb[t][:].indirect(n2_sb[:, lcols]), ACT.Copy)
+                nc.scalar.activation(
+                    ea[:],
+                    y_sb[t][:].indirect(n1_sb[:, lcols]),
+                    ACT.Exp,
+                    bias=bias1[:, t : t + 1],
+                    scale=neg_tau[:, t : t + 1],
+                )
+                nc.vector.scalar_tensor_tensor(
+                    pull, ea[:], neg_2gs[:, t : t + 1], y_n2[:], ALU.mult, ALU.mult
+                )
+                nc.vector.scalar_tensor_tensor(
+                    z_f32[:, t, :], y_sb[t][:, cols], gs_sb[:, t : t + 1], pull, ALU.mult, ALU.add
+                )
+            nc.vector.tensor_copy(
+                z_bf[:].rearrange("p (c i) t -> p c t i", i=4), z_f32[:].rearrange("p t (c i) -> p c t i", i=4)
+            )
+            nc.vector.quantize_mx(
+                out=z_codes[:, cols].bitcast(FP8X4),
+                scales=z_bytes[:, cols],
+                in_=z_bf[:].rearrange("p c t -> p (c t)"),
+            )
+            score(b_ps[0], cb_words, cb_bytes, 0, cols)
+            if h == 0:
+                nc.vector.tensor_scalar(
+                    b_win[0][:, cols], b_ps[0][:, cols], 0.0625, None, ALU.mult, ALU.max, accum_out=top_part[:]
+                )
+            else:
+                nc.vector.tensor_scalar(
+                    b_win[0][:, cols], b_ps[0][:, cols], 0.0625, top_part[:], ALU.mult, ALU.max, accum_out=top[:, 0:1]
+                )
+
+        whole = slice(0, S)
+        ea2 = keep.tile([P, PACK, S], F32, name="ea2", tag="fetched")
+        for t in range(PACK):
+            if t > 0:
+                score(b_ps[t], cb_words, cb_bytes, t, whole)
+                nc.vector.tensor_scalar(
+                    b_win[t][:, whole], b_ps[t][:], 0.0625, None, ALU.mult, ALU.max, accum_out=top[:, t : t + 1]
+                )
+            nc.vector.tensor_tensor(bias2[:, t : t + 1], top[:, t : t + 1], neg_tau2[:, t : t + 1], ALU.mult)
+            nc.scalar.activation(
+                ea2[:, t, :],
+                b_win[t][:].indirect(n3_sb[:]),
+                ACT.Exp,
+                bias=bias2[:, t : t + 1],
+                scale=tau2_sb[:, t : t + 1],
+            )
+
+        ca_words = pick_words(ca_sb, "ca_words")
+        ca_bytes = pick_bytes(ca_sb, "ca_bytes")
+
+        root = keep.tile([P, PACK, S], F32, name="root")
+        weight = keep.tile([P, PACK, S], F32, name="weight")
+        a_sb = []
+        for t in range(PACK):
+            a_ps = psum.tile([P, S], F32, name="a_ps%d" % t, tag="ya%d" % t)
+            score(a_ps, ca_words, ca_bytes, t, whole)
+            a_t = keep.tile([P, S], F32, name="a_sb%d" % t)
+            nc.vector.tensor_scalar(a_t[:], a_ps[:], 0.0625, None, ALU.mult)
+            a_sb.append(a_t)
+        for h in range(2):
+            cols = slice(h * HALF, (h + 1) * HALF)
+            nc.scalar.activation(root[:, :, cols], ea2[:, :, cols], ACT.Abs_reciprocal_sqrt, bias=0.5, scale=2.0)
+            nc.vector.tensor_tensor(weight[:, :, cols], root[:, :, cols], root[:, :, cols], ALU.mult)
+        out_rows = out.rearrange("(p t) c -> p t c", t=PACK)
+        a_n4 = keep.tile([P, PACK, S], F32, name="a_n4", tag="fetched")
+        diff = keep.tile([P, PACK, S], F32, name="diff")
+        res = keep.tile([P, PACK, S], F32, name="res")
+        for t in range(PACK):
+            for h in range(2):
+                cols = slice(h * HALF, (h + 1) * HALF)
+                lcols = slice(h * HALF // 16, (h + 1) * HALF // 16)
+                nc.scalar.activation(a_n4[:, t, cols], a_sb[t][:].indirect(n4_sb[:, lcols]), ACT.Copy)
+            pieces = [whole] if t < PACK - 1 else [slice(0, HALF), slice(HALF, S)]
+            for cols in pieces:
+                nc.vector.tensor_tensor(diff[:, t, cols], a_sb[t][:, cols], a_n4[:, t, cols], ALU.subtract)
+                nc.vector.tensor_tensor(res[:, t, cols], diff[:, t, cols], weight[:, t, cols], ALU.mult)
+            nc.sync.dma_start(out_rows[:, t, :], res[:, t, :])

@@ -18,7 +18,9 @@ ACT = mybir.ActivationFunctionType
 P = 128
 PACK = 4
 HALF = S // 2
-SCALAR_SHARE = 22
+RUN = 4
+SCALAR_SHARE = 44
+TAIL = 128
 
 
 def tile_picked_ccmpqxbebz_none_p_kernel(
@@ -28,7 +30,6 @@ def tile_picked_ccmpqxbebz_none_p_kernel(
     with ExitStack() as ctx:
         lists = ctx.enter_context(tc.tile_pool(name="lists", bufs=1))
         keep = ctx.enter_context(tc.tile_pool(name="keep", bufs=1))
-        ring = ctx.enter_context(tc.tile_pool(name="ring", bufs=3))
         psum = ctx.enter_context(tc.psum_pool(name="psum", bufs=1))
 
         def load_list(src, name):
@@ -51,30 +52,27 @@ def tile_picked_ccmpqxbebz_none_p_kernel(
         for r in range(PACK):
             nc.sync.dma_start(table_bytes[r:P:32, :].bitcast(I32), x_scales[0, r:16:PACK, :].bitcast(I32))
 
-        w_rows = w1.rearrange("(p j) c -> p j c", j=PACK)
-        w_raw = []
-        for u in range(2):
-            raw = keep.tile([P, PACK, H // 2], F32, name="w_raw%d" % u)
-            nc.sync.dma_start(raw[:], w_rows[:, :, u * (H // 2) : (u + 1) * (H // 2)])
-            w_raw.append(raw)
+        w_raw = keep.tile([P, PACK, H], F32, name="w_raw")
+        nc.sync.dma_start(w_raw[:], w1.rearrange("(p j) c -> p j c", j=PACK))
 
         n2_sb = load_list(n2, "n2_sb")
         n1_sb = load_list(n1, "n1_sb")
         tau_sb = load_rows(tau, "tau_sb")
         gs_sb = load_rows(gs, "gs_sb")
         n3_sb = load_list(n3, "n3_sb")
-        tau2_sb = load_rows(tau2, "tau2_sb")
+        tau2_rows = tau2.rearrange("(r t u) o -> t r u o", t=PACK, u=RUN)
+        tau2_sb = []
+        for t in range(PACK):
+            col = keep.tile([P, 1], F32, name="tau2_sb%d" % t)
+            nc.sync.dma_start(col[:], tau2_rows[t])
+            tau2_sb.append(col)
         ca_sb = load_list(ca, "ca_sb")
         n4_sb = load_list(n4, "n4_sb")
 
         def scaled(src, factor, name):
             tl = keep.tile([P, PACK], F32, name=name)
-            nc.gpsimd.tensor_scalar(tl[:], src[:], factor, 0.0, ALU.mult, ALU.add)
+            nc.scalar.activation(tl[:], src[:], ACT.Copy, scale=factor)
             return tl
-
-        neg_tau = scaled(tau_sb, -1.0, "neg_tau")
-        neg_2gs = scaled(gs_sb, -2.0, "neg_2gs")
-        neg_tau2 = scaled(tau2_sb, -1.0, "neg_tau2")
 
         xq_words = keep.tile([P, S], U32, name="xq_words", align_bytes=64)
         xq_bytes = keep.tile([P, S], U8, name="xq_bytes", tag="picked_bytes", align_bytes=64)
@@ -83,26 +81,24 @@ def tile_picked_ccmpqxbebz_none_p_kernel(
 
         def pick_words(list_sb, name):
             words = keep.tile([P, PACK, P], U32, name=name, tag="pair_words", align_bytes=64)
-            nc.vector.tensor_copy(words[:].rearrange("p t m -> p m t"), table_words[:].indirect(list_sb[:]))
+            nc.vector.tensor_copy(words[:].rearrange("p t (r u) -> p r t u", u=RUN), table_words[:].indirect(list_sb[:]))
             return words
 
         def pick_bytes(list_sb, name):
             scale_bytes = keep.tile([P, PACK, P], U8, name=name, tag="picked_bytes", align_bytes=64)
-            nc.vector.tensor_copy(scale_bytes[:].rearrange("p t m -> p m t"), table_bytes[:].indirect(list_sb[:]))
+            nc.vector.tensor_copy(scale_bytes[:].rearrange("p t (r u) -> p r t u", u=RUN), table_bytes[:].indirect(list_sb[:]))
             return scale_bytes
 
         cb_words = pick_words(cb_sb, "cb_words")
 
         w_grouped = keep.tile([P, PACK, P, PACK], BF16, name="w_grouped", align_bytes=64)
 
-        def deal_views(u, m0, m1):
-            dst = w_grouped[:, :, u * 64 + m0 : u * 64 + m1, :].rearrange("p t m j -> p m j t")
-            src = w_raw[u][:, :, PACK * m0 : PACK * m1].rearrange("p j (m t) -> p m j t", t=PACK)
-            return dst, src
-
-        nc.scalar.activation(*deal_views(0, 0, 64), ACT.Copy)
-        nc.scalar.activation(*deal_views(1, 0, SCALAR_SHARE), ACT.Copy)
-        nc.vector.tensor_copy(*deal_views(1, SCALAR_SHARE, 64))
+        w_dealt = w_grouped[:].rearrange("p t m j -> p m j t")
+        w_plain = w_raw[:].rearrange("p j (m t) -> p m j t", t=PACK)
+        nc.scalar.activation(w_dealt[:, :SCALAR_SHARE], w_plain[:, :SCALAR_SHARE], ACT.Copy)
+        nc.vector.tensor_copy(w_dealt[:, SCALAR_SHARE:], w_plain[:, SCALAR_SHARE:])
+        neg_tau = scaled(tau_sb, -1.0, "neg_tau")
+        neg_2gs = scaled(gs_sb, -2.0, "neg_2gs")
         w_codes = keep.tile([P, PACK, P], U32, name="w_codes", align_bytes=64)
         w_bytes = keep.tile([P, PACK, P], U8, name="w_bytes", align_bytes=64)
 
@@ -125,14 +121,15 @@ def tile_picked_ccmpqxbebz_none_p_kernel(
                 start=True,
                 stop=True,
             )
-            y_t = keep.tile([P, S], F32, name="y_sb%d" % t)
-            nc.vector.tensor_scalar(y_t[:], y_ps[:], 1.0, None, ALU.mult, ALU.min, accum_out=low[:, t : t + 1])
+            y_t = keep.tile([P, 2 * S], F32, name="y_sb%d" % t)
+            nc.vector.tensor_scalar(y_t[:, :S], y_ps[:], 1.0, None, ALU.mult, ALU.min, accum_out=low[:, t : t + 1])
             nc.vector.tensor_tensor(bias1[:, t : t + 1], low[:, t : t + 1], tau_sb[:, t : t + 1], ALU.mult)
             y_sb.append(y_t)
 
         cb_bytes = pick_bytes(cb_sb, "cb_bytes")
 
-        b_win = [keep.tile([P, 2 * S], F32, name="b_win%d" % t) for t in range(PACK)]
+        b_win = [keep.tile([P, 2 * S], F32, name="b_win%d" % t, tag="b_win%d" % t) for t in range(PACK)]
+        a_win = [keep.tile([P, 2 * S], F32, name="a_win%d" % t) for t in range(PACK)]
         z_codes = keep.tile([P, S], U32, name="z_codes", align_bytes=64)
         z_bytes = keep.tile([P, S], U8, name="z_bytes", align_bytes=64)
         b_ps = [psum.tile([P, S], F32, name="b_ps%d" % t) for t in range(PACK)]
@@ -151,48 +148,58 @@ def tile_picked_ccmpqxbebz_none_p_kernel(
                 stop=True,
             )
 
-        for h in range(2):
-            cols = slice(h * HALF, (h + 1) * HALF)
-            lcols = slice(h * HALF // 16, (h + 1) * HALF // 16)
-            z_f32 = keep.tile([P, PACK, HALF], F32, name="z_f32_%d" % h)
-            z_bf = keep.tile([P, HALF, PACK], BF16, name="z_bf_%d" % h, align_bytes=64)
-            for t in range(PACK):
-                pull = b_win[t][:, S + h * HALF : S + (h + 1) * HALF]
-                y_n2 = ring.tile([P, HALF], F32, name="y_n2")
-                ea = ring.tile([P, HALF], F32, name="ea")
-                nc.scalar.activation(y_n2[:], y_sb[t][:].indirect(n2_sb[:, lcols]), ACT.Copy)
+        whole = slice(0, S)
+        halves = [slice(0, HALF), slice(HALF, S)]
+        last = PACK - 1
+        y_n2 = keep.tile([P, PACK, S], F32, name="y_n2")
+        pull = keep.tile([P, PACK, S], F32, name="pull")
+        z_f32 = keep.tile([P, PACK, S], F32, name="z_f32")
+        z_bf = keep.tile([P, S, PACK], BF16, name="z_bf", align_bytes=64)
+
+        def entries(list_sb, cols):
+            return list_sb[:, cols.start // 16 : cols.stop // 16]
+
+        for t in range(PACK):
+            pieces = [whole] if t < last else halves
+            ea = a_win[t][:, S:]
+            nc.scalar.activation(y_n2[:, t, :], y_sb[t][:].indirect(n2_sb[:]), ACT.Copy)
+            for cols in pieces:
                 nc.scalar.activation(
-                    ea[:],
-                    y_sb[t][:].indirect(n1_sb[:, lcols]),
+                    ea[:, cols],
+                    y_sb[t][:].indirect(entries(n1_sb, cols)),
                     ACT.Exp,
                     bias=bias1[:, t : t + 1],
                     scale=neg_tau[:, t : t + 1],
                 )
                 nc.vector.scalar_tensor_tensor(
-                    pull, ea[:], neg_2gs[:, t : t + 1], y_n2[:], ALU.mult, ALU.mult
+                    pull[:, t, cols], ea[:, cols], neg_2gs[:, t : t + 1], y_n2[:, t, cols], ALU.mult, ALU.mult
                 )
+            for cols in pieces:
                 nc.vector.scalar_tensor_tensor(
-                    z_f32[:, t, :], y_sb[t][:, cols], gs_sb[:, t : t + 1], pull, ALU.mult, ALU.add
+                    z_f32[:, t, cols], y_sb[t][:, cols], gs_sb[:, t : t + 1], pull[:, t, cols], ALU.mult, ALU.add
                 )
+        for cols in halves:
             nc.vector.tensor_copy(
-                z_bf[:].rearrange("p (c i) t -> p c t i", i=4), z_f32[:].rearrange("p t (c i) -> p c t i", i=4)
+                z_bf[:, cols, :].rearrange("p (c i) t -> p c t i", i=4),
+                z_f32[:, :, cols].rearrange("p t (c i) -> p c t i", i=4),
             )
+        for cols in halves:
             nc.vector.quantize_mx(
                 out=z_codes[:, cols].bitcast(FP8X4),
                 scales=z_bytes[:, cols],
-                in_=z_bf[:].rearrange("p c t -> p (c t)"),
+                in_=z_bf[:, cols, :].rearrange("p c t -> p (c t)"),
             )
-            score(b_ps[0], cb_words, cb_bytes, 0, cols)
-            if h == 0:
-                nc.vector.tensor_scalar(
-                    b_win[0][:, cols], b_ps[0][:, cols], 0.0625, None, ALU.mult, ALU.max, accum_out=top_part[:]
-                )
-            else:
-                nc.vector.tensor_scalar(
-                    b_win[0][:, cols], b_ps[0][:, cols], 0.0625, top_part[:], ALU.mult, ALU.max, accum_out=top[:, 0:1]
-                )
+        first, second = halves
+        b_first = psum.tile([P, S], F32, name="b_first", tag="ya0")
+        score(b_first, cb_words, cb_bytes, 0, first)
+        score(b_ps[0], cb_words, cb_bytes, 0, second)
+        nc.vector.tensor_scalar(
+            b_win[0][:, first], b_first[:, first], 0.0625, None, ALU.mult, ALU.max, accum_out=top_part[:]
+        )
+        nc.vector.tensor_scalar(
+            b_win[0][:, second], b_ps[0][:, second], 0.0625, top_part[:], ALU.mult, ALU.max, accum_out=top[:, 0:1]
+        )
 
-        whole = slice(0, S)
         ea2 = keep.tile([P, PACK, S], F32, name="ea2", tag="fetched")
         for t in range(PACK):
             if t > 0:
@@ -200,42 +207,38 @@ def tile_picked_ccmpqxbebz_none_p_kernel(
                 nc.vector.tensor_scalar(
                     b_win[t][:, whole], b_ps[t][:], 0.0625, None, ALU.mult, ALU.max, accum_out=top[:, t : t + 1]
                 )
-            nc.vector.tensor_tensor(bias2[:, t : t + 1], top[:, t : t + 1], neg_tau2[:, t : t + 1], ALU.mult)
+            nc.vector.tensor_scalar(
+                bias2[:, t : t + 1], top[:, t : t + 1], tau2_sb[t][:], -1.0, ALU.mult, ALU.mult
+            )
             nc.scalar.activation(
                 ea2[:, t, :],
                 b_win[t][:].indirect(n3_sb[:]),
                 ACT.Exp,
                 bias=bias2[:, t : t + 1],
-                scale=tau2_sb[:, t : t + 1],
+                scale=tau2_sb[t][:],
             )
 
         ca_words = pick_words(ca_sb, "ca_words")
         ca_bytes = pick_bytes(ca_sb, "ca_bytes")
 
-        root = keep.tile([P, PACK, S], F32, name="root")
+        root = keep.tile([P, PACK, S], F32, name="root", tag="b_win%d" % last)
         weight = keep.tile([P, PACK, S], F32, name="weight")
-        a_sb = []
+        a_ps = [psum.tile([P, S], F32, name="a_ps%d" % t, tag="ya%d" % t) for t in range(PACK)]
         for t in range(PACK):
-            a_ps = psum.tile([P, S], F32, name="a_ps%d" % t, tag="ya%d" % t)
-            score(a_ps, ca_words, ca_bytes, t, whole)
-            a_t = keep.tile([P, S], F32, name="a_sb%d" % t)
-            nc.vector.tensor_scalar(a_t[:], a_ps[:], 0.0625, None, ALU.mult)
-            a_sb.append(a_t)
-        for h in range(2):
-            cols = slice(h * HALF, (h + 1) * HALF)
-            nc.scalar.activation(root[:, :, cols], ea2[:, :, cols], ACT.Abs_reciprocal_sqrt, bias=0.5, scale=2.0)
-            nc.vector.tensor_tensor(weight[:, :, cols], root[:, :, cols], root[:, :, cols], ALU.mult)
-        out_rows = out.rearrange("(p t) c -> p t c", t=PACK)
+            score(a_ps[t], ca_words, ca_bytes, t, whole)
+            nc.vector.tensor_scalar(a_win[t][:, whole], a_ps[t][:], 0.0625, None, ALU.mult)
+        for pair in (slice(0, 2), slice(2, PACK)):
+            nc.scalar.activation(root[:, pair, :], ea2[:, pair, :], ACT.Abs_reciprocal_sqrt, bias=0.5, scale=2.0)
+            nc.vector.tensor_tensor(weight[:, pair, :], root[:, pair, :], root[:, pair, :], ALU.mult)
+        out_rows = out.rearrange("(r t u) c -> t r u c", t=PACK, u=RUN)
         a_n4 = keep.tile([P, PACK, S], F32, name="a_n4", tag="fetched")
         diff = keep.tile([P, PACK, S], F32, name="diff")
         res = keep.tile([P, PACK, S], F32, name="res")
         for t in range(PACK):
-            for h in range(2):
-                cols = slice(h * HALF, (h + 1) * HALF)
-                lcols = slice(h * HALF // 16, (h + 1) * HALF // 16)
-                nc.scalar.activation(a_n4[:, t, cols], a_sb[t][:].indirect(n4_sb[:, lcols]), ACT.Copy)
-            pieces = [whole] if t < PACK - 1 else [slice(0, HALF), slice(HALF, S)]
-            for cols in pieces:
-                nc.vector.tensor_tensor(diff[:, t, cols], a_sb[t][:, cols], a_n4[:, t, cols], ALU.subtract)
+            for cols in [whole] if t < last else [slice(0, S - TAIL), slice(S - TAIL, S)]:
+                nc.scalar.activation(a_n4[:, t, cols], a_win[t][:].indirect(entries(n4_sb, cols)), ACT.Copy)
+                nc.vector.scalar_tensor_tensor(
+                    diff[:, t, cols], a_ps[t][:, cols], 0.0625, a_n4[:, t, cols], ALU.mult, ALU.subtract
+                )
                 nc.vector.tensor_tensor(res[:, t, cols], diff[:, t, cols], weight[:, t, cols], ALU.mult)
-            nc.sync.dma_start(out_rows[:, t, :], res[:, t, :])
+                nc.sync.dma_start(out_rows[t, :, :, cols], res[:, t, cols])

@@ -45,15 +45,14 @@ def tile_picked_ccmpqxbebz_none_p_kernel(
         table_bytes = keep.tile([P, T], U8, name="table_bytes", align_bytes=64)
         nc.vector.memset(table_bytes[:].bitcast(I32), 0)
 
-        offs_sb = load_list(offs, "offs_sb")
-        cb_sb = load_list(cb, "cb_sb")
         table_words = keep.tile([P, T], U32, name="table_words", align_bytes=64)
         nc.sync.dma_start(table_words[:].bitcast(I32), x_words[0].rearrange("p n r -> p (n r)").bitcast(I32))
-        for r in range(PACK):
-            nc.sync.dma_start(table_bytes[r:P:32, :].bitcast(I32), x_scales[0, r:16:PACK, :].bitcast(I32))
-
+        offs_sb = load_list(offs, "offs_sb")
+        cb_sb = load_list(cb, "cb_sb")
         w_raw = keep.tile([P, PACK, H], F32, name="w_raw")
         nc.sync.dma_start(w_raw[:], w1.rearrange("(p j) c -> p j c", j=PACK))
+        for r in range(PACK):
+            nc.sync.dma_start(table_bytes[r:P:32, :].bitcast(I32), x_scales[0, r:16:PACK, :].bitcast(I32))
 
         n2_sb = load_list(n2, "n2_sb")
         n1_sb = load_list(n1, "n1_sb")
@@ -133,7 +132,7 @@ def tile_picked_ccmpqxbebz_none_p_kernel(
         z_codes = keep.tile([P, S], U32, name="z_codes", align_bytes=64)
         z_bytes = keep.tile([P, S], U8, name="z_bytes", align_bytes=64)
         b_ps = [psum.tile([P, S], F32, name="b_ps%d" % t) for t in range(PACK)]
-        top_part = keep.tile([P, 1], F32, name="top_part")
+        top_first = keep.tile([P, 1], F32, name="top_first")
         top = keep.tile([P, PACK], F32, name="top")
         bias2 = keep.tile([P, PACK], F32, name="bias2")
 
@@ -190,28 +189,35 @@ def tile_picked_ccmpqxbebz_none_p_kernel(
                 in_=z_bf[:, cols, :].rearrange("p c t -> p (c t)"),
             )
         first, second = halves
+        neg_tau2 = keep.tile([P, 1], F32, name="neg_tau2")
+        nc.scalar.activation(neg_tau2[:], tau2_sb[0][:], ACT.Copy, scale=-1.0)
         b_first = psum.tile([P, S], F32, name="b_first", tag="ya0")
         score(b_first, cb_words, cb_bytes, 0, first)
         score(b_ps[0], cb_words, cb_bytes, 0, second)
         nc.vector.tensor_scalar(
-            b_win[0][:, first], b_first[:, first], 0.0625, None, ALU.mult, ALU.max, accum_out=top_part[:]
+            b_win[0][:, first], b_first[:, first], 0.0625, None, ALU.mult, ALU.max, accum_out=top_first[:]
         )
         nc.vector.tensor_scalar(
-            b_win[0][:, second], b_ps[0][:, second], 0.0625, top_part[:], ALU.mult, ALU.max, accum_out=top[:, 0:1]
+            b_win[0][:, second], b_ps[0][:, second], 0.0625, None, ALU.mult, ALU.max, accum_out=top[:, 0:1]
         )
 
-        ea2 = keep.tile([P, PACK, S], F32, name="ea2", tag="fetched")
+        ea2 = [
+            keep.tile([P, 2, S], F32, name="ea2_low", tag="fetched"),
+            keep.tile([P, 2, S], F32, name="ea2_high"),
+        ]
         for t in range(PACK):
             if t > 0:
                 score(b_ps[t], cb_words, cb_bytes, t, whole)
                 nc.vector.tensor_scalar(
                     b_win[t][:, whole], b_ps[t][:], 0.0625, None, ALU.mult, ALU.max, accum_out=top[:, t : t + 1]
                 )
-            nc.vector.tensor_scalar(
-                bias2[:, t : t + 1], top[:, t : t + 1], tau2_sb[t][:], -1.0, ALU.mult, ALU.mult
-            )
+                nc.vector.tensor_scalar(
+                    bias2[:, t : t + 1], top[:, t : t + 1], tau2_sb[t][:], -1.0, ALU.mult, ALU.mult
+                )
+            else:
+                nc.vector.tensor_scalar(bias2[:, 0:1], top[:, 0:1], top_first[:], neg_tau2[:], ALU.max, ALU.mult)
             nc.scalar.activation(
-                ea2[:, t, :],
+                ea2[t // 2][:, t % 2, :],
                 b_win[t][:].indirect(n3_sb[:]),
                 ACT.Exp,
                 bias=bias2[:, t : t + 1],
@@ -221,14 +227,15 @@ def tile_picked_ccmpqxbebz_none_p_kernel(
         ca_words = pick_words(ca_sb, "ca_words")
         ca_bytes = pick_bytes(ca_sb, "ca_bytes")
 
-        root = keep.tile([P, PACK, S], F32, name="root", tag="b_win%d" % last)
+        root = keep.tile([P, PACK, S], F32, name="root", tag="b_win2")
         weight = keep.tile([P, PACK, S], F32, name="weight")
         a_ps = [psum.tile([P, S], F32, name="a_ps%d" % t, tag="ya%d" % t) for t in range(PACK)]
         for t in range(PACK):
             score(a_ps[t], ca_words, ca_bytes, t, whole)
             nc.vector.tensor_scalar(a_win[t][:, whole], a_ps[t][:], 0.0625, None, ALU.mult)
-        for pair in (slice(0, 2), slice(2, PACK)):
-            nc.scalar.activation(root[:, pair, :], ea2[:, pair, :], ACT.Abs_reciprocal_sqrt, bias=0.5, scale=2.0)
+        for i in range(2):
+            pair = slice(2 * i, 2 * i + 2)
+            nc.scalar.activation(root[:, pair, :], ea2[i][:], ACT.Abs_reciprocal_sqrt, bias=0.5, scale=2.0)
             nc.vector.tensor_tensor(weight[:, pair, :], root[:, pair, :], root[:, pair, :], ALU.mult)
         out_rows = out.rearrange("(r t u) c -> t r u c", t=PACK, u=RUN)
         a_n4 = keep.tile([P, PACK, S], F32, name="a_n4", tag="fetched")

from contextlib import ExitStack

import concourse.mybir as mybir

K, T, S, H, C = 512, 2048, 256, 512, 512
FLOPS = 2 * K * S * (H + 2 * C)

F32 = mybir.dt.float32
BF16 = mybir.dt.bfloat16
I32 = mybir.dt.int32
U32 = mybir.dt.uint32
U16 = mybir.dt.uint16
U8 = mybir.dt.uint8
FP8X4 = mybir.dt.float8_e4m3fn_x4
ALU = mybir.AluOpType
ACT = mybir.ActivationFunctionType

P = 128
PACK = 4
HALF = S // 2
RUN = 4
SCALAR_SHARE = 44
TAIL = 128


def tile_picked_ccmpqxbebz_none_p_kernel(
    tc, x_words, x_scales, w1, tau, gs, tau2, offs, n1, n2, ca, cb, n3, n4, out
):
    nc = tc.nc
    with ExitStack() as ctx:
        lists = ctx.enter_context(tc.tile_pool(name="lists", bufs=1))
        keep = ctx.enter_context(tc.tile_pool(name="keep", bufs=1))
        psum = ctx.enter_context(tc.psum_pool(name="psum", bufs=1))

        def load_list(src, name):
            tl = lists.tile(list(src.shape), U16, name=name)
            nc.sync.dma_start(tl[:], src)
            return tl

        def load_rows(src, name):
            tl = keep.tile([P, PACK], F32, name=name)
            nc.sync.dma_start(tl[:], src.rearrange("(p t) o -> p (t o)", t=PACK))
            return tl

        table_bytes = keep.tile([P, T], U8, name="table_bytes", align_bytes=64)
        nc.vector.memset(table_bytes[:].bitcast(I32), 0)

        table_words = keep.tile([P, T], U32, name="table_words", align_bytes=64)
        nc.sync.dma_start(table_words[:].bitcast(I32), x_words[0].rearrange("p n r -> p (n r)").bitcast(I32))
        offs_sb = load_list(offs, "offs_sb")
        cb_sb = load_list(cb, "cb_sb")
        w_raw = keep.tile([P, PACK, H], F32, name="w_raw")
        nc.sync.dma_start(w_raw[:], w1.rearrange("(p j) c -> p j c", j=PACK))
        for r in range(PACK):
            nc.sync.dma_start(table_bytes[r:P:32, :].bitcast(I32), x_scales[0, r:16:PACK, :].bitcast(I32))

        n2_sb = load_list(n2, "n2_sb")
        n1_sb = load_list(n1, "n1_sb")
        tau_sb = load_rows(tau, "tau_sb")
        gs_sb = load_rows(gs, "gs_sb")
        n3_sb = load_list(n3, "n3_sb")
        tau2_rows = tau2.rearrange("(r t u) o -> t r u o", t=PACK, u=RUN)
        tau2_sb = []
        for t in range(PACK):
            col = keep.tile([P, 1], F32, name="tau2_sb%d" % t)
            nc.sync.dma_start(col[:], tau2_rows[t])
            tau2_sb.append(col)
        ca_sb = load_list(ca, "ca_sb")
        n4_sb = load_list(n4, "n4_sb")

        def scaled(src, factor, name):
            tl = keep.tile([P, PACK], F32, name=name)
            nc.scalar.activation(tl[:], src[:], ACT.Copy, scale=factor)
            return tl

        xq_words = keep.tile([P, S], U32, name="xq_words", align_bytes=64)
        xq_bytes = keep.tile([P, S], U8, name="xq_bytes", tag="picked_bytes", align_bytes=64)
        nc.vector.tensor_copy(xq_words[:], table_words[:].indirect(offs_sb[:]))
        nc.vector.tensor_copy(xq_bytes[:], table_bytes[:].indirect(offs_sb[:]))

        def pick_words(list_sb, name):
            words = keep.tile([P, PACK, P], U32, name=name, tag="pair_words", align_bytes=64)
            nc.vector.tensor_copy(words[:].rearrange("p t (r u) -> p r t u", u=RUN), table_words[:].indirect(list_sb[:]))
            return words

        def pick_bytes(list_sb, name):
            scale_bytes = keep.tile([P, PACK, P], U8, name=name, tag="picked_bytes", align_bytes=64)
            nc.vector.tensor_copy(scale_bytes[:].rearrange("p t (r u) -> p r t u", u=RUN), table_bytes[:].indirect(list_sb[:]))
            return scale_bytes

        cb_words = pick_words(cb_sb, "cb_words")

        w_grouped = keep.tile([P, PACK, P, PACK], BF16, name="w_grouped", align_bytes=64)

        w_dealt = w_grouped[:].rearrange("p t m j -> p m j t")
        w_plain = w_raw[:].rearrange("p j (m t) -> p m j t", t=PACK)
        nc.scalar.activation(w_dealt[:, :SCALAR_SHARE], w_plain[:, :SCALAR_SHARE], ACT.Copy)
        nc.vector.tensor_copy(w_dealt[:, SCALAR_SHARE:], w_plain[:, SCALAR_SHARE:])
        neg_tau = scaled(tau_sb, -1.0, "neg_tau")
        neg_2gs = scaled(gs_sb, -2.0, "neg_2gs")
        w_codes = keep.tile([P, PACK, P], U32, name="w_codes", align_bytes=64)
        w_bytes = keep.tile([P, PACK, P], U8, name="w_bytes", align_bytes=64)

        low = keep.tile([P, PACK], F32, name="low")
        bias1 = keep.tile([P, PACK], F32, name="bias1")
        y_sb = []
        for t in range(PACK):
            nc.vector.quantize_mx(
                out=w_codes[:, t, :].bitcast(FP8X4),
                scales=w_bytes[:, t, :],
                in_=w_grouped[:, t, :, :].rearrange("p m j -> p (m j)"),
            )
            y_ps = psum.tile([P, S], F32, name="y_ps%d" % t, tag="ya%d" % t)
            nc.tensor.matmul_mx(
                out=y_ps[:],
                lhsT=w_codes[:, t, :].bitcast(FP8X4),
                lhsT_scale=w_bytes[:, t, :],
                rhs=xq_words[:].bitcast(FP8X4),
                rhs_scale=xq_bytes[:],
                start=True,
                stop=True,
            )
            y_t = keep.tile([P, 2 * S], F32, name="y_sb%d" % t)
            nc.vector.tensor_scalar(y_t[:, :S], y_ps[:], 1.0, None, ALU.mult, ALU.min, accum_out=low[:, t : t + 1])
            nc.vector.tensor_tensor(bias1[:, t : t + 1], low[:, t : t + 1], tau_sb[:, t : t + 1], ALU.mult)
            y_sb.append(y_t)

        cb_bytes = pick_bytes(cb_sb, "cb_bytes")

        b_win = [keep.tile([P, 2 * S], F32, name="b_win%d" % t, tag="b_win%d" % t) for t in range(PACK)]
        a_win = [keep.tile([P, 2 * S], F32, name="a_win%d" % t) for t in range(PACK)]
        z_codes = keep.tile([P, S], U32, name="z_codes", align_bytes=64)
        z_bytes = keep.tile([P, S], U8, name="z_bytes", align_bytes=64)
        b_ps = [psum.tile([P, S], F32, name="b_ps%d" % t) for t in range(PACK)]
        top_first = keep.tile([P, 1], F32, name="top_first")
        top = keep.tile([P, PACK], F32, name="top")
        bias2 = keep.tile([P, PACK], F32, name="bias2")

        def score(ps, words, scale_bytes, t, cols):
            nc.tensor.matmul_mx(
                out=ps[:, cols],
                lhsT=words[:, t, :].bitcast(FP8X4),
                lhsT_scale=scale_bytes[:, t, :],
                rhs=z_codes[:, cols].bitcast(FP8X4),
                rhs_scale=z_bytes[:, cols],
                start=True,
                stop=True,
            )

        whole = slice(0, S)
        halves = [slice(0, HALF), slice(HALF, S)]
        last = PACK - 1
        y_n2 = keep.tile([P, PACK, S], F32, name="y_n2")
        pull = keep.tile([P, PACK, S], F32, name="pull")
        z_f32 = keep.tile([P, PACK, S], F32, name="z_f32")
        z_bf = keep.tile([P, S, PACK], BF16, name="z_bf", align_bytes=64)

        def entries(list_sb, cols):
            return list_sb[:, cols.start // 16 : cols.stop // 16]

        for t in range(PACK):
            pieces = [whole] if t < last else halves
            ea = a_win[t][:, S:]
            nc.scalar.activation(y_n2[:, t, :], y_sb[t][:].indirect(n2_sb[:]), ACT.Copy)
            for cols in pieces:
                nc.scalar.activation(
                    ea[:, cols],
                    y_sb[t][:].indirect(entries(n1_sb, cols)),
                    ACT.Exp,
                    bias=bias1[:, t : t + 1],
                    scale=neg_tau[:, t : t + 1],
                )
                nc.vector.scalar_tensor_tensor(
                    pull[:, t, cols], ea[:, cols], neg_2gs[:, t : t + 1], y_n2[:, t, cols], ALU.mult, ALU.mult
                )
            for cols in pieces:
                nc.vector.scalar_tensor_tensor(
                    z_f32[:, t, cols], y_sb[t][:, cols], gs_sb[:, t : t + 1], pull[:, t, cols], ALU.mult, ALU.add
                )
        for cols in halves:
            nc.vector.tensor_copy(
                z_bf[:, cols, :].rearrange("p (c i) t -> p c t i", i=4),
                z_f32[:, :, cols].rearrange("p t (c i) -> p c t i", i=4),
            )
        for cols in halves:
            nc.vector.quantize_mx(
                out=z_codes[:, cols].bitcast(FP8X4),
                scales=z_bytes[:, cols],
                in_=z_bf[:, cols, :].rearrange("p c t -> p (c t)"),
            )
        first, second = halves
        neg_tau2 = keep.tile([P, 1], F32, name="neg_tau2")
        nc.scalar.activation(neg_tau2[:], tau2_sb[0][:], ACT.Copy, scale=-1.0)
        b_first = psum.tile([P, S], F32, name="b_first", tag="ya0")
        score(b_first, cb_words, cb_bytes, 0, first)
        score(b_ps[0], cb_words, cb_bytes, 0, second)
        nc.vector.tensor_scalar(
            b_win[0][:, first], b_first[:, first], 0.0625, None, ALU.mult, ALU.max, accum_out=top_first[:]
        )
        nc.vector.tensor_scalar(
            b_win[0][:, second], b_ps[0][:, second], 0.0625, None, ALU.mult, ALU.max, accum_out=top[:, 0:1]
        )

        ea2 = [
            keep.tile([P, 2, S], F32, name="ea2_low", tag="fetched"),
            keep.tile([P, 2, S], F32, name="ea2_high"),
        ]
        for t in range(PACK):
            if t > 0:
                score(b_ps[t], cb_words, cb_bytes, t, whole)
                nc.vector.tensor_scalar(
                    b_win[t][:, whole], b_ps[t][:], 0.0625, None, ALU.mult, ALU.max, accum_out=top[:, t : t + 1]
                )
                nc.vector.tensor_scalar(
                    bias2[:, t : t + 1], top[:, t : t + 1], tau2_sb[t][:], -1.0, ALU.mult, ALU.mult
                )
            else:
                nc.vector.tensor_scalar(bias2[:, 0:1], top[:, 0:1], top_first[:], neg_tau2[:], ALU.max, ALU.mult)
            nc.scalar.activation(
                ea2[t // 2][:, t % 2, :],
                b_win[t][:].indirect(n3_sb[:]),
                ACT.Exp,
                bias=bias2[:, t : t + 1],
                scale=tau2_sb[t][:],
            )

        ca_words = pick_words(ca_sb, "ca_words")
        ca_bytes = pick_bytes(ca_sb, "ca_bytes")

        root = keep.tile([P, PACK, S], F32, name="root", tag="b_win2")
        weight = keep.tile([P, PACK, S], F32, name="weight")
        a_ps = [psum.tile([P, S], F32, name="a_ps%d" % t, tag="ya%d" % t) for t in range(PACK)]
        for t in range(PACK):
            score(a_ps[t], ca_words, ca_bytes, t, whole)
            nc.vector.tensor_scalar(a_win[t][:, whole], a_ps[t][:], 0.0625, None, ALU.mult)
        for i in range(2):
            pair = slice(2 * i, 2 * i + 2)
            nc.scalar.activation(root[:, pair, :], ea2[i][:], ACT.Abs_reciprocal_sqrt, bias=0.5, scale=2.0)
            nc.vector.tensor_tensor(weight[:, pair, :], root[:, pair, :], root[:, pair, :], ALU.mult)
        out_rows = out.rearrange("(r t u) c -> t r u c", t=PACK, u=RUN)
        a_n4 = keep.tile([P, PACK, S], F32, name="a_n4", tag="fetched")
        diff = keep.tile([P, PACK, S], F32, name="diff")
        res = keep.tile([P, PACK, S], F32, name="res")
        for t in range(PACK):
            for cols in [whole] if t < last else [slice(0, S - TAIL), slice(S - TAIL, S)]:
                nc.scalar.activation(a_n4[:, t, cols], a_win[t][:].indirect(entries(n4_sb, cols)), ACT.Copy)
                nc.vector.scalar_tensor_tensor(
                    diff[:, t, cols], a_ps[t][:, cols], 0.0625, a_n4[:, t, cols], ALU.mult, ALU.subtract
                )
                nc.vector.tensor_tensor(res[:, t, cols], diff[:, t, cols], weight[:, t, cols], ALU.mult)
                nc.sync.dma_start(out_rows[t, :, :, cols], res[:, t, cols])
